import numpy as np
import ml_dtypes


def mxq(x, axis, fmt="e4m3"):
    dtype, down = {"e4m3": (ml_dtypes.float8_e4m3fn, 7), "e5m2": (ml_dtypes.float8_e5m2, 14)}[fmt]
    v = np.moveaxis(np.asarray(x, np.float32).astype(ml_dtypes.bfloat16).astype(np.float64), axis, -1)
    blocks = v.reshape(v.shape[:-1] + (-1, 32))
    amax = np.abs(blocks).max(-1, keepdims=True)
    byte = np.maximum(np.where(amax > 0, np.frexp(amax)[1] - 1 + 127, 0) - down, 1)
    scale = np.exp2(byte - 127.0)
    codes = (blocks / scale).astype(np.float32).astype(dtype).astype(np.float64)
    return np.moveaxis((codes * scale).reshape(v.shape), -1, axis)


WIDE = False


def mx_kscale(k):
    if not WIDE:
        return np.ones(k)
    levels = np.array([10, -10, 5, -5, 0])
    if k % 512:
        return np.exp2(np.random.permutation(np.resize(levels, k // 32))).repeat(32)
    a = np.empty((k // 512, 16))
    for p in range(k // 512):
        a[p, :8] = np.random.permutation(np.resize(levels, 8))
        for g in range(8):
            far = levels[np.abs(levels - a[p, g]) >= 10]
            a[p, g + 8] = far[np.random.randint(len(far))]
    return np.exp2(a.ravel()).repeat(32)


def f64(x):
    return np.asarray(x).astype(np.float64)


def striped(idx):
    return np.tile(idx.reshape(-1, 16).T, (8, 1)).astype(np.uint16)


def unstriped(offs):
    return offs[:16].T.reshape(-1).astype(np.int64)


def pack_weight(w):
    k, n = w.shape
    w = f64(np.asarray(w, np.float32).astype(ml_dtypes.bfloat16)).reshape(k // 32, 32, n)
    amax = np.abs(w).max(1)
    byte = np.clip(np.where(amax > 0, np.frexp(amax)[1] - 1 + 127 - 7, 1), 1, 254)
    scaled = (w * np.exp2(127.0 - byte)[:, None, :]).reshape(k, n).astype(np.float32)
    words = np.ascontiguousarray(scaled.reshape(k // 512, 128, 4, n).transpose(0, 1, 3, 2)).astype(ml_dtypes.float8_e4m3fn).view(np.uint8)
    return words, np.ascontiguousarray(byte.astype(np.uint8).reshape(k // 512, 16, n))


def unpack_weight(words, scales):
    g, p, n, _ = words.shape
    vals = np.ascontiguousarray(words).view(ml_dtypes.float8_e4m3fn).astype(np.float64) * np.repeat(np.exp2(scales.astype(np.float64) - 127.0), 8, axis=1)[..., None]
    return vals.transpose(0, 1, 3, 2).reshape(g * 512, n)


def gelu(v):
    return 0.5 * v * (1.0 + np.tanh(np.sqrt(2.0 / np.pi) * (v + 0.044715 * v**3)))


K, T, S, V, N = 1024, 1024, 512, 256, 128


def setup_inputs():
    n = np.random.standard_normal
    s = mx_kscale(K)[:, None]
    packed_w1 = pack_weight(n((K, N)) / np.sqrt(K) / s)
    return {
        "xT": (n((K, T)) * s).astype(np.float32),
        "w1_words": packed_w1[0],
        "w1_scales": packed_w1[1],
        "offs": striped(np.random.permutation(T)[:S]),
        "pos1": striped(np.random.permutation(S)[:V]),
        "pos2": striped(np.random.permutation(S)[:V]),
        "pos3": striped(np.random.permutation(S)[:V]),
    }


def reference(xT, w1_words, w1_scales, offs, pos1, pos2, pos3):
    xq = mxq(f64(xT)[:, unstriped(offs)], 0, "e4m3")
    y = gelu(unpack_weight(w1_words, w1_scales).T @ xq)
    n0 = y[:, unstriped(pos1)]
    n1 = y[:, unstriped(pos2)]
    n2 = y[:, unstriped(pos3)]
    return np.maximum(np.minimum(n0, n1), np.minimum(np.maximum(n0, n1), n2))

@@ -1,0 +1,132 @@
+from contextlib import ExitStack
+
+import concourse.mybir as mybir
+
+K, T, S, V, N = 1024, 1024, 512, 256, 128
+FLOPS = 2 * K * N * S
+
+F32 = mybir.dt.float32
+BF16 = mybir.dt.bfloat16
+I32 = mybir.dt.int32
+U32 = mybir.dt.uint32
+U16 = mybir.dt.uint16
+U8 = mybir.dt.uint8
+FP8X4 = mybir.dt.float8_e4m3fn_x4
+GELU = mybir.ActivationFunctionType.Gelu_apprx_tanh
+MAX = mybir.AluOpType.max
+MIN = mybir.AluOpType.min
+
+P = 128
+K_PASS = 512
+PASSES = K // K_PASS
+CHUNK = 512
+SCALAR_SHARE = 192
+HALF = S // 2
+
+
+def tile_picked_median_gelu_e_kernel(tc, xT, w1_words, w1_scales, offs, pos1, pos2, pos3, out):
+    nc = tc.nc
+    with ExitStack() as ctx:
+        keep = ctx.enter_context(tc.tile_pool(name="keep", bufs=1))
+        psum = ctx.enter_context(tc.psum_pool(name="psum", bufs=1))
+
+        offs_sb = keep.tile([P, S // 16], U16, name="offs_sb")
+        pos_sb = [keep.tile([P, V // 16], U16, name=f"pos_sb{i}") for i in range(3)]
+
+        zero = keep.tile([P, 1], F32, name="zero")
+        nc.vector.memset(zero[:], 0.0)
+        zero_bias = keep.tile([P, 1], F32, name="zero_bias")
+        nc.scalar.activation(zero_bias[:], zero[:], GELU)
+
+        w_scales = keep.tile([P, PASSES * N], U8, name="w_scales", align_bytes=64)
+        nc.gpsimd.memset(w_scales[:], 0)
+        for q in range(4):
+            nc.gpsimd.dma_start(
+                out=w_scales[32 * q : 32 * q + 4, :].bitcast(I32).rearrange("r (z c) -> r z c", z=PASSES),
+                in_=w1_scales[:, 4 * q : 4 * q + 4, :].bitcast(I32).rearrange("z r c -> r z c"),
+            )
+
+        raw = {}
+        for z in range(PASSES):
+            rows = xT[z * K_PASS : (z + 1) * K_PASS, :].rearrange("(p t) c -> p t c", t=4)
+            for u in range(2):
+                for h in range(T // CHUNK):
+                    raw[z, u, h] = keep.tile([P, 2, CHUNK], F32, name=f"raw{z}{u}{h}")
+                    nc.sync.dma_start(out=raw[z, u, h][:], in_=rows[:, 2 * u : 2 * u + 2, h * CHUNK : (h + 1) * CHUNK])
+                    if (z, u, h) == (0, 0, 0):
+                        nc.sync.dma_start(offs_sb[:], offs)
+        w_words = keep.tile([P, PASSES * N], U32, name="w_words", align_bytes=64)
+        nc.sync.dma_start(
+            out=w_words[:].bitcast(I32).rearrange("p (z n) -> p z n", z=PASSES),
+            in_=w1_words.rearrange("z p n t -> p z (n t)").bitcast(I32),
+        )
+        for tile, src in zip(pos_sb, (pos1, pos2, pos3)):
+            nc.sync.dma_start(tile[:], src)
+
+        def round_pairs(z, u):
+            pairs = keep.tile([P, 2 * T], BF16, name=f"pairs{z}{u}")
+            view = pairs[:].rearrange("p (c e) -> p c e", e=2)
+            first = raw[z, u, 0][:].rearrange("p e c -> p c e")
+            second = raw[z, u, 1][:].rearrange("p e c -> p c e")
+            nc.scalar.copy(view[:, 0:CHUNK, :], first)
+            nc.scalar.copy(view[:, CHUNK : CHUNK + SCALAR_SHARE, :], second[:, 0:SCALAR_SHARE, :])
+            nc.vector.tensor_copy(view[:, CHUNK + SCALAR_SHARE : T, :], second[:, SCALAR_SHARE:CHUNK, :])
+            return pairs
+
+        def gather_pairs(pairs, picked, u, lo, hi):
+            dst = picked[:].bitcast(U32).rearrange("p (j u) -> p j u", u=2)
+            nc.vector.tensor_copy(dst[:, :, u], pairs[:].bitcast(U32).indirect(offs_sb[:, lo // 16 : hi // 16]))
+
+        def quantise(picked, n, name):
+            codes = keep.tile([P, n], U32, name="codes" + name, align_bytes=64)
+            scales = keep.tile([P, n], U8, name="scales" + name, align_bytes=64)
+            nc.vector.quantize_mx(out=codes[:].bitcast(FP8X4), scales=scales[:], in_=picked[:])
+            return codes, scales
+
+        acc = [psum.tile([P, HALF], F32, name=f"acc{h}") for h in range(2)]
+
+        def product(h, z, codes, scales):
+            nc.tensor.matmul_mx(
+                out=acc[h][:],
+                lhsT=w_words[:, z * N : (z + 1) * N].bitcast(FP8X4),
+                lhsT_scale=w_scales[:, z * N : (z + 1) * N],
+                rhs=codes.bitcast(FP8X4),
+                rhs_scale=scales,
+                start=(z == 0),
+                stop=(z == PASSES - 1),
+            )
+
+        picked0 = keep.tile([P, 4 * S], BF16, name="picked0", align_bytes=64)
+        picked1 = [keep.tile([P, 4 * HALF], BF16, name=f"picked1{h}", align_bytes=64) for h in range(2)]
+        for u in range(2):
+            gather_pairs(round_pairs(0, u), picked0, u, 0, S)
+        pairs10 = round_pairs(1, 0)
+        codes0, scales0 = quantise(picked0, S, "0")
+        for h in range(2):
+            product(h, 0, codes0[:, h * HALF : (h + 1) * HALF], scales0[:, h * HALF : (h + 1) * HALF])
+        for h in range(2):
+            gather_pairs(pairs10, picked1[h], 0, h * HALF, (h + 1) * HALF)
+        pairs11 = round_pairs(1, 1)
+        for h in range(2):
+            gather_pairs(pairs11, picked1[h], 1, h * HALF, (h + 1) * HALF)
+        y = keep.tile([P, S], F32, name="y")
+        for h in range(2):
+            codes1, scales1 = quantise(picked1[h], HALF, f"1{h}")
+            product(h, 1, codes1[:], scales1[:])
+            nc.scalar.activation(y[:, h * HALF : (h + 1) * HALF], acc[h][:], GELU, bias=zero_bias[:])
+
+        nb = [keep.tile([P, V], F32, name=f"nb{i}") for i in range(3)]
+        for i in range(3):
+            nc.vector.tensor_copy(nb[i][:], y[:].indirect(pos_sb[i][:]))
+        larger = keep.tile([P, V], F32, name="larger")
+        smaller = keep.tile([P, V], F32, name="smaller")
+        nc.vector.tensor_tensor(larger[:], nb[0][:], nb[1][:], MAX)
+        nc.vector.tensor_tensor(smaller[:], nb[0][:], nb[1][:], MIN)
+        capped = [keep.tile([P, V // 2], F32, name=f"capped{h}") for h in range(2)]
+        median = [keep.tile([P, V // 2], F32, name=f"median{h}") for h in range(2)]
+        cols = [slice(h * V // 2, (h + 1) * V // 2) for h in range(2)]
+        for h in range(2):
+            nc.vector.tensor_tensor(capped[h][:], larger[:, cols[h]], nb[2][:, cols[h]], MIN)
+        for h, queue in enumerate((nc.scalar, nc.sync)):
+            nc.vector.tensor_tensor(median[h][:], smaller[:, cols[h]], capped[h][:], MAX)
+            queue.dma_start(out=out[:, cols[h]], in_=median[h][:])

@@ -19,9 +19,14 @@ MIN = mybir.AluOpType.min
 P = 128
 K_PASS = 512
 PASSES = K // K_PASS
-CHUNK = 512
-SCALAR_SHARE = 192
-HALF = S // 2
+LOADS = {
+    (0, 0): [(1024, 448)],
+    (0, 1): [(512, 512), (512, 192)],
+    (1, 0): [(384, 384), (384, 384), (256, 256)],
+    (1, 1): [(512, 512), (512, 192)],
+}
+GROUP = 128
+GROUPS = S // GROUP
 
 
 def tile_picked_median_gelu_e_kernel(tc, xT, w1_words, w1_scales, offs, pos1, pos2, pos3, out):
@@ -39,20 +44,17 @@ def tile_picked_median_gelu_e_kernel(tc, xT, w1_words, w1_scales, offs, pos1, po
         nc.scalar.activation(zero_bias[:], zero[:], GELU)
 
         w_scales = keep.tile([P, PASSES * N], U8, name="w_scales", align_bytes=64)
-        nc.gpsimd.memset(w_scales[:], 0)
-        for q in range(4):
-            nc.gpsimd.dma_start(
-                out=w_scales[32 * q : 32 * q + 4, :].bitcast(I32).rearrange("r (z c) -> r z c", z=PASSES),
-                in_=w1_scales[:, 4 * q : 4 * q + 4, :].bitcast(I32).rearrange("z r c -> r z c"),
-            )
+        nc.vector.memset(w_scales[:].bitcast(I32), 0)
 
         raw = {}
         for z in range(PASSES):
             rows = xT[z * K_PASS : (z + 1) * K_PASS, :].rearrange("(p t) c -> p t c", t=4)
             for u in range(2):
-                for h in range(T // CHUNK):
-                    raw[z, u, h] = keep.tile([P, 2, CHUNK], F32, name=f"raw{z}{u}{h}")
-                    nc.sync.dma_start(out=raw[z, u, h][:], in_=rows[:, 2 * u : 2 * u + 2, h * CHUNK : (h + 1) * CHUNK])
+                c0 = 0
+                for h, (width, share) in enumerate(LOADS[z, u]):
+                    raw[z, u, h] = keep.tile([P, 2, width], F32, name=f"raw{z}{u}{h}")
+                    nc.sync.dma_start(out=raw[z, u, h][:], in_=rows[:, 2 * u : 2 * u + 2, c0 : c0 + width])
+                    c0 = c0 + width
                     if (z, u, h) == (0, 0, 0):
                         nc.sync.dma_start(offs_sb[:], offs)
         w_words = keep.tile([P, PASSES * N], U32, name="w_words", align_bytes=64)
@@ -60,34 +62,41 @@ def tile_picked_median_gelu_e_kernel(tc, xT, w1_words, w1_scales, offs, pos1, po
             out=w_words[:].bitcast(I32).rearrange("p (z n) -> p z n", z=PASSES),
             in_=w1_words.rearrange("z p n t -> p z (n t)").bitcast(I32),
         )
+        for q in range(4):
+            nc.sync.dma_start(
+                out=w_scales[32 * q : 32 * q + 4, :].bitcast(I32).rearrange("r (z c) -> r z c", z=PASSES),
+                in_=w1_scales[:, 4 * q : 4 * q + 4, :].bitcast(I32).rearrange("z r c -> r z c"),
+            )
         for tile, src in zip(pos_sb, (pos1, pos2, pos3)):
             nc.sync.dma_start(tile[:], src)
 
         def round_pairs(z, u):
             pairs = keep.tile([P, 2 * T], BF16, name=f"pairs{z}{u}")
             view = pairs[:].rearrange("p (c e) -> p c e", e=2)
-            first = raw[z, u, 0][:].rearrange("p e c -> p c e")
-            second = raw[z, u, 1][:].rearrange("p e c -> p c e")
-            nc.scalar.copy(view[:, 0:CHUNK, :], first)
-            nc.scalar.copy(view[:, CHUNK : CHUNK + SCALAR_SHARE, :], second[:, 0:SCALAR_SHARE, :])
-            nc.vector.tensor_copy(view[:, CHUNK + SCALAR_SHARE : T, :], second[:, SCALAR_SHARE:CHUNK, :])
+            c0 = 0
+            for h, (width, share) in enumerate(LOADS[z, u]):
+                src = raw[z, u, h][:].rearrange("p e c -> p c e")
+                if share > 0:
+                    nc.scalar.copy(view[:, c0 : c0 + share, :], src[:, 0:share, :])
+                if share < width:
+                    nc.vector.tensor_copy(view[:, c0 + share : c0 + width, :], src[:, share:width, :])
+                c0 = c0 + width
             return pairs
 
-        def gather_pairs(pairs, picked, u, lo, hi):
-            dst = picked[:].bitcast(U32).rearrange("p (j u) -> p j u", u=2)
-            nc.vector.tensor_copy(dst[:, :, u], pairs[:].bitcast(U32).indirect(offs_sb[:, lo // 16 : hi // 16]))
+        def gather(dst, pairs, lo, hi):
+            nc.vector.tensor_copy(dst, pairs[:].bitcast(U32).indirect(offs_sb[:, lo // 16 : hi // 16]))
 
-        def quantise(picked, n, name):
+        def quantise(woven, n, name):
             codes = keep.tile([P, n], U32, name="codes" + name, align_bytes=64)
             scales = keep.tile([P, n], U8, name="scales" + name, align_bytes=64)
-            nc.vector.quantize_mx(out=codes[:].bitcast(FP8X4), scales=scales[:], in_=picked[:])
+            nc.vector.quantize_mx(out=codes[:].bitcast(FP8X4), scales=scales[:], in_=woven[:])
             return codes, scales
 
-        acc = [psum.tile([P, HALF], F32, name=f"acc{h}") for h in range(2)]
+        acc = [psum.tile([P, GROUP], F32, name=f"acc{g}") for g in range(GROUPS)]
 
-        def product(h, z, codes, scales):
+        def product(g, z, codes, scales):
             nc.tensor.matmul_mx(
-                out=acc[h][:],
+                out=acc[g][:],
                 lhsT=w_words[:, z * N : (z + 1) * N].bitcast(FP8X4),
                 lhsT_scale=w_scales[:, z * N : (z + 1) * N],
                 rhs=codes.bitcast(FP8X4),
@@ -96,24 +105,30 @@ def tile_picked_median_gelu_e_kernel(tc, xT, w1_words, w1_scales, offs, pos1, po
                 stop=(z == PASSES - 1),
             )
 
-        picked0 = keep.tile([P, 4 * S], BF16, name="picked0", align_bytes=64)
-        picked1 = [keep.tile([P, 4 * HALF], BF16, name=f"picked1{h}", align_bytes=64) for h in range(2)]
+        woven0 = keep.tile([P, 4 * S], BF16, name="woven0", align_bytes=64)
         for u in range(2):
-            gather_pairs(round_pairs(0, u), picked0, u, 0, S)
+            gather(woven0[:].bitcast(U32).rearrange("p (j u) -> p j u", u=2)[:, :, u], round_pairs(0, u), 0, S)
+        codes0, scales0 = quantise(woven0, S, "0")
+        for g in range(GROUPS):
+            product(g, 0, codes0[:, g * GROUP : (g + 1) * GROUP], scales0[:, g * GROUP : (g + 1) * GROUP])
+        picked1 = [keep.tile([P, 2 * GROUP], U32, name=f"picked1{g}") for g in range(GROUPS)]
         pairs10 = round_pairs(1, 0)
-        codes0, scales0 = quantise(picked0, S, "0")
-        for h in range(2):
-            product(h, 0, codes0[:, h * HALF : (h + 1) * HALF], scales0[:, h * HALF : (h + 1) * HALF])
-        for h in range(2):
-            gather_pairs(pairs10, picked1[h], 0, h * HALF, (h + 1) * HALF)
+        for g in range(GROUPS):
+            gather(picked1[g][:, 0:GROUP], pairs10, g * GROUP, (g + 1) * GROUP)
         pairs11 = round_pairs(1, 1)
-        for h in range(2):
-            gather_pairs(pairs11, picked1[h], 1, h * HALF, (h + 1) * HALF)
+        woven1 = [keep.tile([P, 4 * GROUP], BF16, name=f"woven1{g}", align_bytes=64) for g in range(GROUPS)]
+        for g in range(GROUPS):
+            gather(picked1[g][:, GROUP : 2 * GROUP], pairs11, g * GROUP, (g + 1) * GROUP)
+            nc.scalar.copy(
+                woven1[g][:].bitcast(U32).rearrange("p (j u) -> p j u", u=2),
+                picked1[g][:].rearrange("p (u j) -> p j u", u=2),
+            )
         y = keep.tile([P, S], F32, name="y")
-        for h in range(2):
-            codes1, scales1 = quantise(picked1[h], HALF, f"1{h}")
-            product(h, 1, codes1[:], scales1[:])
-            nc.scalar.activation(y[:, h * HALF : (h + 1) * HALF], acc[h][:], GELU, bias=zero_bias[:])
+        for g in range(GROUPS):
+            codes1, scales1 = quantise(woven1[g], GROUP, f"1{g}")
+            product(g, 1, codes1[:], scales1[:])
+        for g in range(GROUPS):
+            nc.scalar.activation(y[:, g * GROUP : (g + 1) * GROUP], acc[g][:], GELU, bias=zero_bias[:])
 
         nb = [keep.tile([P, V], F32, name=f"nb{i}") for i in range(3)]
         for i in range(3):

@@ -105,12 +105,22 @@ def tile_picked_median_gelu_e_kernel(tc, xT, w1_words, w1_scales, offs, pos1, po
                 stop=(z == PASSES - 1),
             )
 
-        woven0 = keep.tile([P, 4 * S], BF16, name="woven0", align_bytes=64)
+        half = S // 2
+        picked0 = [keep.tile([P, 2 * half], U32, name=f"picked0{h}") for h in range(2)]
         for u in range(2):
-            gather(woven0[:].bitcast(U32).rearrange("p (j u) -> p j u", u=2)[:, :, u], round_pairs(0, u), 0, S)
-        codes0, scales0 = quantise(woven0, S, "0")
-        for g in range(GROUPS):
-            product(g, 0, codes0[:, g * GROUP : (g + 1) * GROUP], scales0[:, g * GROUP : (g + 1) * GROUP])
+            pairs = round_pairs(0, u)
+            for h in range(2):
+                gather(picked0[h][:, u * half : (u + 1) * half], pairs, h * half, (h + 1) * half)
+        woven0 = [keep.tile([P, 4 * half], BF16, name=f"woven0{h}", align_bytes=64) for h in range(2)]
+        for h in range(2):
+            nc.vector.tensor_copy(
+                woven0[h][:].bitcast(I32).rearrange("p (j u) -> p j u", u=2),
+                picked0[h][:].bitcast(I32).rearrange("p (u j) -> p j u", u=2),
+            )
+        for h in range(2):
+            codes0, scales0 = quantise(woven0[h], half, f"0{h}")
+            for i in range(2):
+                product(2 * h + i, 0, codes0[:, i * GROUP : (i + 1) * GROUP], scales0[:, i * GROUP : (i + 1) * GROUP])
         picked1 = [keep.tile([P, 2 * GROUP], U32, name=f"picked1{g}") for g in range(GROUPS)]
         pairs10 = round_pairs(1, 0)
         for g in range(GROUPS):

from contextlib import ExitStack

import concourse.mybir as mybir

K, T, S, V, N = 1024, 1024, 512, 256, 128
FLOPS = 2 * K * N * S

F32 = mybir.dt.float32
BF16 = mybir.dt.bfloat16
I32 = mybir.dt.int32
U32 = mybir.dt.uint32
U16 = mybir.dt.uint16
U8 = mybir.dt.uint8
FP8X4 = mybir.dt.float8_e4m3fn_x4
GELU = mybir.ActivationFunctionType.Gelu_apprx_tanh
MAX = mybir.AluOpType.max
MIN = mybir.AluOpType.min

P = 128
K_PASS = 512
PASSES = K // K_PASS
LOADS = {
    (0, 0): [(1024, 448)],
    (0, 1): [(512, 512), (512, 192)],
    (1, 0): [(384, 384), (384, 384), (256, 256)],
    (1, 1): [(512, 512), (512, 192)],
}
GROUP = 128
GROUPS = S // GROUP


def tile_picked_median_gelu_e_kernel(tc, xT, w1_words, w1_scales, offs, pos1, pos2, pos3, out):
    nc = tc.nc
    with ExitStack() as ctx:
        keep = ctx.enter_context(tc.tile_pool(name="keep", bufs=1))
        psum = ctx.enter_context(tc.psum_pool(name="psum", bufs=1))

        offs_sb = keep.tile([P, S // 16], U16, name="offs_sb")
        pos_sb = [keep.tile([P, V // 16], U16, name=f"pos_sb{i}") for i in range(3)]

        zero = keep.tile([P, 1], F32, name="zero")
        nc.vector.memset(zero[:], 0.0)
        zero_bias = keep.tile([P, 1], F32, name="zero_bias")
        nc.scalar.activation(zero_bias[:], zero[:], GELU)

        w_scales = keep.tile([P, PASSES * N], U8, name="w_scales", align_bytes=64)
        nc.vector.memset(w_scales[:].bitcast(I32), 0)

        raw = {}
        for z in range(PASSES):
            rows = xT[z * K_PASS : (z + 1) * K_PASS, :].rearrange("(p t) c -> p t c", t=4)
            for u in range(2):
                c0 = 0
                for h, (width, share) in enumerate(LOADS[z, u]):
                    raw[z, u, h] = keep.tile([P, 2, width], F32, name=f"raw{z}{u}{h}")
                    nc.sync.dma_start(out=raw[z, u, h][:], in_=rows[:, 2 * u : 2 * u + 2, c0 : c0 + width])
                    c0 = c0 + width
                    if (z, u, h) == (0, 0, 0):
                        nc.sync.dma_start(offs_sb[:], offs)
        w_words = keep.tile([P, PASSES * N], U32, name="w_words", align_bytes=64)
        nc.sync.dma_start(
            out=w_words[:].bitcast(I32).rearrange("p (z n) -> p z n", z=PASSES),
            in_=w1_words.rearrange("z p n t -> p z (n t)").bitcast(I32),
        )
        for q in range(4):
            nc.sync.dma_start(
                out=w_scales[32 * q : 32 * q + 4, :].bitcast(I32).rearrange("r (z c) -> r z c", z=PASSES),
                in_=w1_scales[:, 4 * q : 4 * q + 4, :].bitcast(I32).rearrange("z r c -> r z c"),
            )
        for tile, src in zip(pos_sb, (pos1, pos2, pos3)):
            nc.sync.dma_start(tile[:], src)

        def round_pairs(z, u):
            pairs = keep.tile([P, 2 * T], BF16, name=f"pairs{z}{u}")
            view = pairs[:].rearrange("p (c e) -> p c e", e=2)
            c0 = 0
            for h, (width, share) in enumerate(LOADS[z, u]):
                src = raw[z, u, h][:].rearrange("p e c -> p c e")
                if share > 0:
                    nc.scalar.copy(view[:, c0 : c0 + share, :], src[:, 0:share, :])
                if share < width:
                    nc.vector.tensor_copy(view[:, c0 + share : c0 + width, :], src[:, share:width, :])
                c0 = c0 + width
            return pairs

        def gather(dst, pairs, lo, hi):
            nc.vector.tensor_copy(dst, pairs[:].bitcast(U32).indirect(offs_sb[:, lo // 16 : hi // 16]))

        def quantise(woven, n, name):
            codes = keep.tile([P, n], U32, name="codes" + name, align_bytes=64)
            scales = keep.tile([P, n], U8, name="scales" + name, align_bytes=64)
            nc.vector.quantize_mx(out=codes[:].bitcast(FP8X4), scales=scales[:], in_=woven[:])
            return codes, scales

        acc = [psum.tile([P, GROUP], F32, name=f"acc{g}") for g in range(GROUPS)]

        def product(g, z, codes, scales):
            nc.tensor.matmul_mx(
                out=acc[g][:],
                lhsT=w_words[:, z * N : (z + 1) * N].bitcast(FP8X4),
                lhsT_scale=w_scales[:, z * N : (z + 1) * N],
                rhs=codes.bitcast(FP8X4),
                rhs_scale=scales,
                start=(z == 0),
                stop=(z == PASSES - 1),
            )

        half = S // 2
        picked0 = [keep.tile([P, 2 * half], U32, name=f"picked0{h}") for h in range(2)]
        for u in range(2):
            pairs = round_pairs(0, u)
            for h in range(2):
                gather(picked0[h][:, u * half : (u + 1) * half], pairs, h * half, (h + 1) * half)
        woven0 = [keep.tile([P, 4 * half], BF16, name=f"woven0{h}", align_bytes=64) for h in range(2)]
        for h in range(2):
            nc.vector.tensor_copy(
                woven0[h][:].bitcast(I32).rearrange("p (j u) -> p j u", u=2),
                picked0[h][:].bitcast(I32).rearrange("p (u j) -> p j u", u=2),
            )
        for h in range(2):
            codes0, scales0 = quantise(woven0[h], half, f"0{h}")
            for i in range(2):
                product(2 * h + i, 0, codes0[:, i * GROUP : (i + 1) * GROUP], scales0[:, i * GROUP : (i + 1) * GROUP])
        picked1 = [keep.tile([P, 2 * GROUP], U32, name=f"picked1{g}") for g in range(GROUPS)]
        pairs10 = round_pairs(1, 0)
        for g in range(GROUPS):
            gather(picked1[g][:, 0:GROUP], pairs10, g * GROUP, (g + 1) * GROUP)
        pairs11 = round_pairs(1, 1)
        woven1 = [keep.tile([P, 4 * GROUP], BF16, name=f"woven1{g}", align_bytes=64) for g in range(GROUPS)]
        for g in range(GROUPS):
            gather(picked1[g][:, GROUP : 2 * GROUP], pairs11, g * GROUP, (g + 1) * GROUP)
            nc.scalar.copy(
                woven1[g][:].bitcast(U32).rearrange("p (j u) -> p j u", u=2),
                picked1[g][:].rearrange("p (u j) -> p j u", u=2),
            )
        y = keep.tile([P, S], F32, name="y")
        for g in range(GROUPS):
            codes1, scales1 = quantise(woven1[g], GROUP, f"1{g}")
            product(g, 1, codes1[:], scales1[:])
        for g in range(GROUPS):
            nc.scalar.activation(y[:, g * GROUP : (g + 1) * GROUP], acc[g][:], GELU, bias=zero_bias[:])

        nb = [keep.tile([P, V], F32, name=f"nb{i}") for i in range(3)]
        for i in range(3):
            nc.vector.tensor_copy(nb[i][:], y[:].indirect(pos_sb[i][:]))
        larger = keep.tile([P, V], F32, name="larger")
        smaller = keep.tile([P, V], F32, name="smaller")
        nc.vector.tensor_tensor(larger[:], nb[0][:], nb[1][:], MAX)
        nc.vector.tensor_tensor(smaller[:], nb[0][:], nb[1][:], MIN)
        capped = [keep.tile([P, V // 2], F32, name=f"capped{h}") for h in range(2)]
        median = [keep.tile([P, V // 2], F32, name=f"median{h}") for h in range(2)]
        cols = [slice(h * V // 2, (h + 1) * V // 2) for h in range(2)]
        for h in range(2):
            nc.vector.tensor_tensor(capped[h][:], larger[:, cols[h]], nb[2][:, cols[h]], MIN)
        for h, queue in enumerate((nc.scalar, nc.sync)):
            nc.vector.tensor_tensor(median[h][:], smaller[:, cols[h]], capped[h][:], MAX)
            queue.dma_start(out=out[:, cols[h]], in_=median[h][:])
